import numpy as np
import ml_dtypes


def mxq(x, axis, fmt="e4m3"):
    dtype, down = {"e4m3": (ml_dtypes.float8_e4m3fn, 7), "e5m2": (ml_dtypes.float8_e5m2, 14)}[fmt]
    v = np.moveaxis(np.asarray(x, np.float32).astype(ml_dtypes.bfloat16).astype(np.float64), axis, -1)
    blocks = v.reshape(v.shape[:-1] + (-1, 32))
    amax = np.abs(blocks).max(-1, keepdims=True)
    byte = np.maximum(np.where(amax > 0, np.frexp(amax)[1] - 1 + 127, 0) - down, 1)
    scale = np.exp2(byte - 127.0)
    codes = (blocks / scale).astype(np.float32).astype(dtype).astype(np.float64)
    return np.moveaxis((codes * scale).reshape(v.shape), -1, axis)


WIDE = False


def mx_kscale(k):
    if not WIDE:
        return np.ones(k)
    levels = np.array([30, -30])
    if k % 512:
        return np.exp2(np.random.permutation(np.resize(levels, k // 32))).repeat(32)
    a = np.empty((k // 512, 16))
    for p in range(k // 512):
        a[p, :8] = np.random.permutation(np.resize(levels, 8))
        for g in range(8):
            far = levels[np.abs(levels - a[p, g]) >= 10]
            a[p, g + 8] = far[np.random.randint(len(far))]
    return np.exp2(a.ravel()).repeat(32)


BF16 = ml_dtypes.bfloat16


def bf(x):
    return np.asarray(x, np.float32).astype(BF16)


def f64(x):
    return np.asarray(x).astype(np.float64)


E2M1 = np.array([0.0, 0.5, 1.0, 1.5, 2.0, 3.0, 4.0, 6.0, -0.0, -0.5, -1.0, -1.5, -2.0, -3.0, -4.0, -6.0])


def pack_weight(w, fmt):
    k, n = w.shape
    w = f64(bf(w)).reshape(k // 32, 32, n)
    amax = np.abs(w).max(1)
    if fmt == "e4m3":
        byte = np.frexp(amax)[1] - 1 + 127 - 7
    else:
        mant, ex = np.frexp(amax / 6.0)
        byte = np.where(mant > 0.5, ex, ex - 1) + 127
    byte = np.clip(np.where(amax > 0, byte, 1), 1, 254)
    scaled = (w * np.exp2(127.0 - byte)[:, None, :]).reshape(k, n).astype(np.float32)
    by_word = np.ascontiguousarray(scaled.reshape(k // 512, 128, 4, n).transpose(0, 1, 3, 2))
    if fmt == "e4m3":
        words = by_word.astype(ml_dtypes.float8_e4m3fn).view(np.uint8)
    else:
        c = by_word.astype(ml_dtypes.float4_e2m1fn).view(np.uint8) & 0xF
        words = c[..., 0::2] | (c[..., 1::2] << 4)
    return np.ascontiguousarray(words), np.ascontiguousarray(byte.astype(np.uint8).reshape(k // 512, 16, n))


def unpack_weight(words, scales, fmt):
    g, p, n, _ = words.shape
    if fmt == "e4m3":
        vals = np.ascontiguousarray(words).view(ml_dtypes.float8_e4m3fn).astype(np.float64)
    else:
        nib = np.empty((g, p, n, 4), np.uint8)
        nib[..., 0::2] = words & 0xF
        nib[..., 1::2] = words >> 4
        vals = E2M1[nib]
    vals = vals * np.repeat(np.exp2(scales.astype(np.float64) - 127.0), 8, axis=1)[..., None]
    return vals.transpose(0, 1, 3, 2).reshape(g * 512, n)
def pack4(w):
    words, scales = pack_weight(w, "e2m1")
    return words.reshape(words.shape[0], 128, -1), scales


def unpack4(words, scales):
    return unpack_weight(words.reshape(words.shape[0], 128, -1, 2), scales, "e2m1")


M, K, N, D = 1024, 2048, 1024, 2048


def setup_inputs():
    s = mx_kscale(K)
    t = mx_kscale(N)
    context = np.random.standard_normal((M, K)) * s
    w = np.random.standard_normal((K, N)) / np.sqrt(K) / s[:, None] * t
    w_words, w_scales = pack4(w)
    turn = np.random.standard_normal((M, N)) * t
    gate = 0.5 + np.random.random(M)
    docs = np.random.standard_normal((D, N)) / np.sqrt(N) / t
    prior = 0.4 * np.random.standard_normal(D)
    return {"context": bf(context), "w_words": w_words, "w_scales": w_scales,
            "turn": bf(turn), "gate": bf(gate), "docs": bf(docs), "prior": bf(prior)}


def reference(context, w_words, w_scales, turn, gate, docs, prior):
    delta = mxq(f64(context), 1, "e4m3") @ unpack4(w_words, w_scales)
    rewritten = f64(turn) + f64(gate)[:, None] * delta
    match = mxq(rewritten, 1, "e5m2") @ mxq(f64(docs), 1, "e4m3").T
    return match + f64(prior)

@@ -1,0 +1,297 @@
+from contextlib import ExitStack
+
+import concourse.mybir as mybir
+from concourse.masks import make_identity
+
+M, K, N, D = 1024, 2048, 1024, 2048
+FLOPS = 2 * M * K * N + 2 * M * N * D
+
+F32 = mybir.dt.float32
+BF16 = mybir.dt.bfloat16
+I32 = mybir.dt.int32
+U32 = mybir.dt.uint32
+U8 = mybir.dt.uint8
+E4M3X4 = mybir.dt.float8_e4m3fn_x4
+E5M2X4 = mybir.dt.float8_e5m2_x4
+E2M1X4 = mybir.dt.float4_e2m1fn_x4
+ADD = mybir.AluOpType.add
+MULT = mybir.AluOpType.mult
+
+P = 128
+BANK = 512
+M_TILES = M // P
+K_PASSES = K // BANK
+N_PASSES = N // BANK
+D_GROUPS = D // 256
+D_CHUNKS = D // BANK
+
+QUANT_LAG = 2
+DOC_PLAN = [0, 1, 2, 2, 2, 1, 0, 0, 0]
+BEFORE = [4] * 8 + [32]
+AFTER = [1] * 8 + [32]
+SORT_AT = 0
+HEAD = [(0,), (1,), (2, 3)]
+HALVES = [(0, 1), (2, 3)]
+PRIOR_AT = [2, 2]
+DOC_SORT = [None] + ["V"] * 7
+CTX_SORT = [None, "V"] + ["S"] * 6
+
+
+def tile_query_rewrite_scoring_s9_kernel(tc, context, w_words, w_scales, turn, gate, docs, prior, out):
+    nc = tc.nc
+    with ExitStack() as ctx:
+        keep = ctx.enter_context(tc.tile_pool(name="keep", bufs=1))
+        work = ctx.enter_context(tc.tile_pool(name="work", bufs=4))
+        psum = ctx.enter_context(tc.psum_pool(name="psum", bufs=8))
+        ctx.enter_context(tc.manual_schedule())
+
+        context_rows = context.rearrange("(p i) k -> i p k", i=M_TILES)
+        turn_rows = turn.rearrange("(p i) n -> i p n", i=M_TILES)
+        out_rows = out.rearrange("(p i) d -> i p d", i=M_TILES)
+        doc_rows = docs.rearrange("(q p e) n -> q p (e n)", p=P, e=2)
+
+        w_scale = keep.tile([P, K_PASSES * N], U8, name="w_scale", align_bytes=64)
+        nc.vector.memset(w_scale[:].bitcast(I32), 0)
+
+        def load(name, shape, dtype, source, queue=nc.sync):
+            tile = keep.tile(shape, dtype, name=name, align_bytes=64)
+            queue.dma_start(out=tile[:], in_=source)
+            return tile
+
+        prior_rows = load("prior_rows", [P, D // P], BF16, prior.rearrange("(p c) -> p c", p=P))
+        ident = keep.tile([P, P], F32, name="ident")
+        make_identity(nc, ident[:])
+
+        def load_w(passes):
+            first, count = passes[0], len(passes)
+            tile = keep.tile([P, count, 2 * N], U8, name="w_codes%d" % first, align_bytes=64)
+            source = w_words[first : first + count].rearrange("g p b -> p g b")
+            nc.sync.dma_start(out=tile[:].bitcast(I32), in_=source.bitcast(I32))
+            for g in passes:
+                w_codes[g] = tile[:, g - first, :]
+
+        def load_ctx(i):
+            tile = load("ctx%d" % i, [P, K], BF16, context_rows[i])
+            ctx_raw[i, HALVES[0]], ctx_raw[i, HALVES[1]] = tile[:, : K // 2], tile[:, K // 2 :]
+
+        ctx_raw, turn_raw, doc_raw, w_codes = {}, {}, {}, {}
+        ctx_raw[0, (0,)] = load("ctx0_first", [P, BANK], BF16, context_rows[0][:, :BANK])
+        load_w((0,))
+        rest = load("ctx0_rest", [P, K - BANK], BF16, context_rows[0][:, BANK:])
+        ctx_raw[0, (1,)], ctx_raw[0, (2, 3)] = rest[:, :BANK], rest[:, BANK:]
+        load_w((1, 2, 3))
+        for q in range(4):
+            nc.scalar.dma_start(
+                out=w_scale[32 * q : 32 * q + 4, :].bitcast(I32).rearrange("r (g n) -> r g n", g=K_PASSES),
+                in_=w_scales[:, 4 * q : 4 * q + 4, :].rearrange("g r n -> r g n").bitcast(I32),
+            )
+        gate_cols = load("gate_cols", [P, M_TILES], BF16, gate.rearrange("(p i) -> p i", p=P), nc.gpsimd)
+        load_ctx(1)
+        doc_steps = []
+        group = 0
+        for count in DOC_PLAN:
+            doc_steps.append(list(range(group, group + count)))
+            group = group + count
+        for s in range(1, M_TILES + 1):
+            if 1 < s < M_TILES:
+                load_ctx(s)
+            turn_raw[s - 1] = load("turn%d" % (s - 1), [P, N], BF16, turn_rows[s - 1])
+            for q in doc_steps[s]:
+                doc_raw[q] = load("docs%d" % q, [P, 2 * N], BF16, doc_rows[q])
+
+        prior_all = keep.tile([P, D], BF16, name="prior_all", align_bytes=64)
+        doc_codes, doc_scale = {}, {}
+        for j in range(D_CHUNKS):
+            for g in range(N_PASSES):
+                doc_codes[j, g] = keep.tile([P, BANK], U32, name="doc_codes%d_%d" % (j, g), align_bytes=64)
+                doc_scale[j, g] = keep.tile([P, BANK], U8, name="doc_scale%d_%d" % (j, g), align_bytes=64)
+        ctx_codes, ctx_scale, rw_codes, rw_scale, rw_sorted, sorted_words = {}, {}, {}, {}, {}, {}
+        pending = []
+
+        def new_bank():
+            return psum.tile([P, BANK], F32, name="bank")
+
+        def flush(lag):
+            for entry in pending:
+                entry[0] = entry[0] + 1
+            while pending and pending[0][0] > lag:
+                pending.pop(0)[1]()
+
+        def ensure(key):
+            while any(entry[2] == key for entry in pending):
+                pending.pop(0)[1]()
+
+        def sort_words(key, raw, engine):
+            words = raw.bitcast(F32)
+            n = words.shape[1]
+            tile = work.tile([P, n], F32, name="sorted", tag="sorted%d" % n)
+            source = words.rearrange("p (j u) -> p u j", u=2)
+            target = tile[:].rearrange("p (u j) -> p u j", u=2)
+            if engine == "S":
+                nc.scalar.copy(out=target, in_=source)
+            else:
+                nc.vector.tensor_copy(out=target, in_=source)
+            sorted_words[key] = tile
+
+        def word_columns(key, raw, first, u):
+            if key in sorted_words:
+                tile = sorted_words[key]
+                start = u * (tile.shape[1] // 2) + first // 2
+                return tile[:, start : start + P]
+            return raw.bitcast(F32)[:, first + u : first + 2 * P : 2]
+
+        def turn_over(key, sources, order, codes, scales, dtype):
+            bank = new_bank()
+            for slot, source in enumerate(sources):
+                nc.tensor.transpose(bank[:, slot * P : (slot + 1) * P], source, ident[:])
+            width = len(sources) * P
+            grouped = work.tile([P, 2 * width], BF16, name="grouped", tag="grouped", bufs=6, align_bytes=64)
+            nc.scalar.copy(
+                out=grouped[:].bitcast(F32).rearrange(order[1], r=P, u=2),
+                in_=bank[:, :width].rearrange(order[0], r=P, u=2),
+            )
+            flush(QUANT_LAG)
+            pending.append([0, lambda: nc.vector.quantize_mx(out=codes.bitcast(dtype), scales=scales, in_=grouped[:]), key])
+
+        BY_PASS = ("p (a u r) -> p a r u", "p (a r u) -> p a r u")
+        BY_ROW = ("p (a u r) -> p r a u", "p (r a u) -> p r a u")
+
+        def ctx_unit(i, passes):
+            codes = work.tile([P, len(passes) * P], U32, name="ctx_codes", tag="ctx_codes", bufs=6, align_bytes=64)
+            scales = work.tile([P, len(passes) * P], U8, name="ctx_scale", tag="ctx_scale", bufs=6, align_bytes=64)
+            for a, g in enumerate(passes):
+                ctx_codes[i, g], ctx_scale[i, g] = codes[:, a * P : (a + 1) * P], scales[:, a * P : (a + 1) * P]
+            key = ("c", i, passes)
+            sources = [word_columns(key, ctx_raw[i, passes][:], 2 * P * a, u) for a in range(len(passes)) for u in range(2)]
+            turn_over(key, sources, BY_PASS, codes[:], scales[:], E4M3X4)
+
+        def doc_unit(q, g):
+            cols = slice((q % 2) * 2 * P, (q % 2 + 1) * 2 * P)
+            sources = [word_columns(("d", q), doc_raw[q][:], (N // 2) * e + 2 * P * g, u) for e in range(2) for u in range(2)]
+            turn_over(("d", q // 2), sources, BY_ROW, doc_codes[q // 2, g][:, cols], doc_scale[q // 2, g][:, cols], E4M3X4)
+
+        def rw_unit(i):
+            codes = keep.tile([P, 2 * P], U32, name="rw_codes%d" % i, align_bytes=64)
+            scales = keep.tile([P, 2 * P], U8, name="rw_scale%d" % i, align_bytes=64)
+            rw_codes[i], rw_scale[i] = codes, scales
+            words = rw_sorted[i][:].bitcast(F32)
+            turn_over(("r", i), [words[:, slot * P : (slot + 1) * P] for slot in range(4)], BY_PASS, codes[:], scales[:], E5M2X4)
+
+        def prior_unit(b):
+            bank = new_bank()
+            words = prior_rows[:].bitcast(F32)
+            for c in range(4):
+                nc.tensor.transpose(bank[:, c * P : (c + 1) * P], words[:, 4 * b + c : 4 * b + c + 1].to_broadcast([P, P]), ident[:])
+            nc.vector.tensor_copy(
+                out=prior_all[:].bitcast(F32).rearrange("m (p c) -> m p c", c=8)[:, :, 4 * b : 4 * b + 4],
+                in_=bank[:].rearrange("m (c p) -> m p c", c=4),
+            )
+
+        def delta_pass(bank, i, half, g):
+            for passes in HEAD + HALVES:
+                if g in passes:
+                    ensure(("c", i, passes))
+            nc.tensor.matmul_mx(
+                out=bank[:],
+                lhsT=ctx_codes[i, g].bitcast(E4M3X4),
+                lhsT_scale=ctx_scale[i, g],
+                rhs=w_codes[g][:, 2 * BANK * half : 2 * BANK * (half + 1)].bitcast(E2M1X4),
+                rhs_scale=w_scale[:, g * N + BANK * half : g * N + BANK * (half + 1)],
+                start=(g == 0),
+                stop=(g == K_PASSES - 1),
+            )
+
+        def rewrite(bank, i, half):
+            if half == 0:
+                rw_sorted[i] = work.tile([P, N], BF16, name="rw_sorted", tag="rw_sorted", bufs=3)
+            cols = slice(half * BANK, (half + 1) * BANK)
+            for u in range(2):
+                nc.vector.scalar_tensor_tensor(
+                    out=rw_sorted[i][:, cols].rearrange("p (u j e) -> p u j e", u=2, e=2)[:, u],
+                    in0=bank[:].rearrange("p (j u e) -> p u j e", u=2, e=2)[:, u],
+                    scalar=gate_cols[:, i : i + 1],
+                    in1=turn_raw[i][:, cols].rearrange("p (j u e) -> p u j e", u=2, e=2)[:, u],
+                    op0=MULT,
+                    op1=ADD,
+                )
+
+        def delta_unit(i, half):
+            bank = new_bank()
+            for g in range(K_PASSES):
+                delta_pass(bank, i, half, g)
+            flush(QUANT_LAG)
+            rewrite(bank, i, half)
+
+        def score_unit(i, j):
+            ensure(("r", i))
+            ensure(("d", j))
+            bank = new_bank()
+            for g in range(N_PASSES):
+                nc.tensor.matmul_mx(
+                    out=bank[:],
+                    lhsT=rw_codes[i][:, g * P : (g + 1) * P].bitcast(E5M2X4),
+                    lhsT_scale=rw_scale[i][:, g * P : (g + 1) * P],
+                    rhs=doc_codes[j, g][:].bitcast(E4M3X4),
+                    rhs_scale=doc_scale[j, g][:],
+                    start=(g == 0),
+                    stop=(g == N_PASSES - 1),
+                )
+            flush(QUANT_LAG)
+            cols = slice(j * BANK, (j + 1) * BANK)
+            scores = work.tile([P, BANK], F32, name="scores", tag="scores", bufs=16)
+            nc.vector.tensor_tensor(out=scores[:], in0=bank[:], in1=prior_all[:, cols], op=ADD)
+            nc.sync.dma_start(out=out_rows[i][:, cols], in_=scores[:])
+
+        def sort_ctx(i):
+            if i < M_TILES and CTX_SORT[i]:
+                for passes in HALVES:
+                    sort_words(("c", i, passes), ctx_raw[i, passes][:], CTX_SORT[i])
+
+        def sort_docs(s):
+            for q in doc_steps[s]:
+                if DOC_SORT[q]:
+                    sort_words(("d", q), doc_raw[q][:], DOC_SORT[q])
+
+        prior_unit(0)
+        ctx_unit(0, (0,))
+        flush(-1)
+        prior_unit(1)
+        for passes in HEAD[1:]:
+            ctx_unit(0, passes)
+        banks = [new_bank(), new_bank()]
+        for g in range(K_PASSES):
+            for half in range(2):
+                delta_pass(banks[half], 0, half, g)
+        sort_ctx(1)
+        for half in range(2):
+            rewrite(banks[half], 0, half)
+        sort_docs(1)
+
+        scored = []
+
+        def score_some(count, tiles, chunks):
+            ready = [(i, j) for i in range(tiles) for j in range(chunks) if (i, j) not in scored]
+            for i, j in ready[:count]:
+                scored.append((i, j))
+                score_unit(i, j)
+
+        for s in range(1, M_TILES + 1):
+            if s < M_TILES:
+                for passes in HALVES:
+                    ctx_unit(s, passes)
+            for q in doc_steps[s]:
+                doc_unit(q, 0)
+                doc_unit(q, 1)
+            rw_unit(s - 1)
+            sort_ctx(s + 1)
+            score_some(BEFORE[s], s - 1, sum(DOC_PLAN[:s]) // 2)
+            if s < M_TILES:
+                if SORT_AT == 0:
+                    flush(QUANT_LAG - 1)
+                    sort_docs(s + 1)
+                delta_unit(s, 0)
+                if SORT_AT == 1:
+                    sort_docs(s + 1)
+                delta_unit(s, 1)
+            score_some(AFTER[s], s, sum(DOC_PLAN[: s + 1]) // 2)
+        assert len(scored) == 32

@@ -25,16 +25,25 @@ N_PASSES = N // BANK
 D_GROUPS = D // 256
 D_CHUNKS = D // BANK
 
-QUANT_LAG = 2
-DOC_PLAN = [0, 1, 2, 2, 2, 1, 0, 0, 0]
-BEFORE = [4] * 8 + [32]
-AFTER = [1] * 8 + [32]
+EARLY = 1
+WARM = 0
+WARM2 = 0
+SORT0 = 1
+UP = 1
 SORT_AT = 0
-HEAD = [(0,), (1,), (2, 3)]
+VS = 1
+TAIL0 = 0
+MID = 3
+RUN = 3
+DOC_BANKS = 4
+DOC_FIRST = 1
+HOLD = 3
+LEAD = 1
+LAST_PARTS = 2
 HALVES = [(0, 1), (2, 3)]
-PRIOR_AT = [2, 2]
-DOC_SORT = [None] + ["V"] * 7
-CTX_SORT = [None, "V"] + ["S"] * 6
+W_LOADS = [(0, 1), (2, 3)]
+DOC_SORT = "V"
+MOST = 4
 
 
 def tile_query_rewrite_scoring_s9_kernel(tc, context, w_words, w_scales, turn, gate, docs, prior, out):
@@ -48,19 +57,35 @@ def tile_query_rewrite_scoring_s9_kernel(tc, context, w_words, w_scales, turn, g
         context_rows = context.rearrange("(p i) k -> i p k", i=M_TILES)
         turn_rows = turn.rearrange("(p i) n -> i p n", i=M_TILES)
         out_rows = out.rearrange("(p i) d -> i p d", i=M_TILES)
-        doc_rows = docs.rearrange("(q p e) n -> q p (e n)", p=P, e=2)
+        doc_rows = docs.rearrange("(q e p) n -> q p e n", p=P, e=2)
 
         w_scale = keep.tile([P, K_PASSES * N], U8, name="w_scale", align_bytes=64)
         nc.vector.memset(w_scale[:].bitcast(I32), 0)
+        if WARM:
+            zeros = keep.tile([P, 864], U32, name="warm_zeros", align_bytes=64)
+            nc.vector.memset(zeros[:], 0)
+            moving, moving_scale = zeros[:, :512], zeros[:, 512:640].bitcast(U8)
+            fixed, fixed_scale = zeros[:, 640:768], zeros[:, 768:800].bitcast(U8)
+            source = zeros[:, 800:864].bitcast(BF16)
+            nc.vector.quantize_mx(out=moving[:, :32].bitcast(E4M3X4), scales=moving_scale[:, :32], in_=source)
+            nc.vector.quantize_mx(out=fixed[:, :32].bitcast(E5M2X4), scales=fixed_scale[:, :32], in_=source)
+
+        def warm_up(count):
+            if count:
+                bank = new_bank()
+            for n in range(count):
+                nc.tensor.matmul_mx(
+                    out=bank[:], lhsT=fixed.bitcast(E5M2X4), lhsT_scale=fixed_scale, rhs=moving.bitcast(E4M3X4), rhs_scale=moving_scale,
+                    start=(n == 0), stop=(n == count - 1),
+                )
+
+        ident = keep.tile([P, P], F32, name="ident")
+        make_identity(nc, ident[:])
 
         def load(name, shape, dtype, source, queue=nc.sync):
             tile = keep.tile(shape, dtype, name=name, align_bytes=64)
             queue.dma_start(out=tile[:], in_=source)
             return tile
-
-        prior_rows = load("prior_rows", [P, D // P], BF16, prior.rearrange("(p c) -> p c", p=P))
-        ident = keep.tile([P, P], F32, name="ident")
-        make_identity(nc, ident[:])
 
         def load_w(passes):
             first, count = passes[0], len(passes)
@@ -72,32 +97,35 @@ def tile_query_rewrite_scoring_s9_kernel(tc, context, w_words, w_scales, turn, g
 
         def load_ctx(i):
             tile = load("ctx%d" % i, [P, K], BF16, context_rows[i])
-            ctx_raw[i, HALVES[0]], ctx_raw[i, HALVES[1]] = tile[:, : K // 2], tile[:, K // 2 :]
+            for passes in HALVES:
+                ctx_raw[i, passes] = tile[:, BANK * passes[0] : BANK * (passes[-1] + 1)]
+
+        doc_banks = [(2 * j + e, g) for j in range(D_CHUNKS) for g in range(N_PASSES) for e in range(2)]
+        doc_steps = {s: [] for s in range(M_TILES + 2)}
+        for n, bank_id in enumerate(doc_banks):
+            doc_steps[DOC_FIRST + n // DOC_BANKS].append(bank_id)
 
         ctx_raw, turn_raw, doc_raw, w_codes = {}, {}, {}, {}
         ctx_raw[0, (0,)] = load("ctx0_first", [P, BANK], BF16, context_rows[0][:, :BANK])
-        load_w((0,))
+        prior_rows = load("prior_rows", [P, D // P], BF16, prior.rearrange("(p c) -> p c", p=P), nc.scalar)
         rest = load("ctx0_rest", [P, K - BANK], BF16, context_rows[0][:, BANK:])
+        load_w(W_LOADS[0])
         ctx_raw[0, (1,)], ctx_raw[0, (2, 3)] = rest[:, :BANK], rest[:, BANK:]
-        load_w((1, 2, 3))
         for q in range(4):
             nc.scalar.dma_start(
                 out=w_scale[32 * q : 32 * q + 4, :].bitcast(I32).rearrange("r (g n) -> r g n", g=K_PASSES),
                 in_=w_scales[:, 4 * q : 4 * q + 4, :].rearrange("g r n -> r g n").bitcast(I32),
             )
-        gate_cols = load("gate_cols", [P, M_TILES], BF16, gate.rearrange("(p i) -> p i", p=P), nc.gpsimd)
         load_ctx(1)
-        doc_steps = []
-        group = 0
-        for count in DOC_PLAN:
-            doc_steps.append(list(range(group, group + count)))
-            group = group + count
-        for s in range(1, M_TILES + 1):
-            if 1 < s < M_TILES:
-                load_ctx(s)
-            turn_raw[s - 1] = load("turn%d" % (s - 1), [P, N], BF16, turn_rows[s - 1])
-            for q in doc_steps[s]:
-                doc_raw[q] = load("docs%d" % q, [P, 2 * N], BF16, doc_rows[q])
+        load_w(W_LOADS[1])
+        gate_cols = load("gate_cols", [P, M_TILES], BF16, gate.rearrange("(p i) -> p i", p=P))
+        for s in range(M_TILES):
+            turn_raw[s] = load("turn%d" % s, [P, N], BF16, turn_rows[s])
+            for q, g in doc_steps[s]:
+                if g == 0:
+                    doc_raw[q] = load("docs%d" % q, [P, 2, N], BF16, doc_rows[q])
+            if s + 2 < M_TILES:
+                load_ctx(s + 2)
 
         prior_all = keep.tile([P, D], BF16, name="prior_all", align_bytes=64)
         doc_codes, doc_scale = {}, {}
@@ -111,86 +139,83 @@ def tile_query_rewrite_scoring_s9_kernel(tc, context, w_words, w_scales, turn, g
         def new_bank():
             return psum.tile([P, BANK], F32, name="bank")
 
-        def flush(lag):
-            for entry in pending:
-                entry[0] = entry[0] + 1
-            while pending and pending[0][0] > lag:
+        def quantise_pending(count):
+            for n in range(min(count, len(pending))):
                 pending.pop(0)[1]()
 
         def ensure(key):
-            while any(entry[2] == key for entry in pending):
-                pending.pop(0)[1]()
+            while any(entry[0] == key for entry in pending):
+                quantise_pending(1)
 
-        def sort_words(key, raw, engine):
-            words = raw.bitcast(F32)
-            n = words.shape[1]
-            tile = work.tile([P, n], F32, name="sorted", tag="sorted%d" % n)
-            source = words.rearrange("p (j u) -> p u j", u=2)
-            target = tile[:].rearrange("p (u j) -> p u j", u=2)
-            if engine == "S":
-                nc.scalar.copy(out=target, in_=source)
-            else:
-                nc.vector.tensor_copy(out=target, in_=source)
-            sorted_words[key] = tile
+        def sort_ctx(i, copy, parts=HALVES):
+            for passes in parts:
+                tile = work.tile([P, BANK], F32, name="ctx_sorted", tag="ctx_sorted")
+                copy(
+                    out=tile[:].rearrange("p (a u c i) -> p a c u i", a=2, u=2, i=4),
+                    in_=ctx_raw[i, passes].bitcast(F32).rearrange("p (a c i u) -> p a c u i", a=2, u=2, i=4),
+                )
+                sorted_words["c", i, passes] = tile
 
-        def word_columns(key, raw, first, u):
-            if key in sorted_words:
-                tile = sorted_words[key]
-                start = u * (tile.shape[1] // 2) + first // 2
-                return tile[:, start : start + P]
-            return raw.bitcast(F32)[:, first + u : first + 2 * P : 2]
+        def sort_docs(s):
+            copy = nc.vector.tensor_copy if DOC_SORT == "V" else nc.scalar.copy
+            for q, g in doc_steps[s]:
+                tile = work.tile([P, BANK], F32, name="doc_sorted", tag="doc_sorted", bufs=2 * DOC_BANKS)
+                copy(
+                    out=tile[:].rearrange("p (a u c i) -> p a c u i", a=2, u=2, i=8),
+                    in_=doc_raw[q][:, :, BANK * g : BANK * (g + 1)].bitcast(F32).rearrange("p a (c u i) -> p a c u i", u=2, i=8),
+                )
+                sorted_words["d", q, g] = tile
 
-        def turn_over(key, sources, order, codes, scales, dtype):
+        def turn_over(key, sources, codes, scales, dtype):
             bank = new_bank()
             for slot, source in enumerate(sources):
                 nc.tensor.transpose(bank[:, slot * P : (slot + 1) * P], source, ident[:])
             width = len(sources) * P
             grouped = work.tile([P, 2 * width], BF16, name="grouped", tag="grouped", bufs=6, align_bytes=64)
             nc.scalar.copy(
-                out=grouped[:].bitcast(F32).rearrange(order[1], r=P, u=2),
-                in_=bank[:, :width].rearrange(order[0], r=P, u=2),
+                out=grouped[:].bitcast(F32).rearrange("p (a r u) -> p a r u", r=P, u=2),
+                in_=bank[:, :width].rearrange("p (a u r) -> p a r u", r=P, u=2),
             )
-            flush(QUANT_LAG)
-            pending.append([0, lambda: nc.vector.quantize_mx(out=codes.bitcast(dtype), scales=scales, in_=grouped[:]), key])
+            pending.append((key, lambda: nc.vector.quantize_mx(out=codes.bitcast(dtype), scales=scales, in_=grouped[:])))
 
-        BY_PASS = ("p (a u r) -> p a r u", "p (a r u) -> p a r u")
-        BY_ROW = ("p (a u r) -> p r a u", "p (r a u) -> p r a u")
+        def quarters(words):
+            return [words[:, slot * P : (slot + 1) * P] for slot in range(4)]
 
         def ctx_unit(i, passes):
             codes = work.tile([P, len(passes) * P], U32, name="ctx_codes", tag="ctx_codes", bufs=6, align_bytes=64)
             scales = work.tile([P, len(passes) * P], U8, name="ctx_scale", tag="ctx_scale", bufs=6, align_bytes=64)
             for a, g in enumerate(passes):
                 ctx_codes[i, g], ctx_scale[i, g] = codes[:, a * P : (a + 1) * P], scales[:, a * P : (a + 1) * P]
-            key = ("c", i, passes)
-            sources = [word_columns(key, ctx_raw[i, passes][:], 2 * P * a, u) for a in range(len(passes)) for u in range(2)]
-            turn_over(key, sources, BY_PASS, codes[:], scales[:], E4M3X4)
+            if ("c", i, passes) not in sorted_words:
+                words = ctx_raw[i, passes][:].bitcast(F32)
+                sources = [words[:, 2 * P * a + u : 2 * P * (a + 1) : 2] for a in range(len(passes)) for u in range(2)]
+            else:
+                sources = quarters(sorted_words["c", i, passes])
+            turn_over(("c", i, passes[0]), sources, codes[:], scales[:], E4M3X4)
 
         def doc_unit(q, g):
             cols = slice((q % 2) * 2 * P, (q % 2 + 1) * 2 * P)
-            sources = [word_columns(("d", q), doc_raw[q][:], (N // 2) * e + 2 * P * g, u) for e in range(2) for u in range(2)]
-            turn_over(("d", q // 2), sources, BY_ROW, doc_codes[q // 2, g][:, cols], doc_scale[q // 2, g][:, cols], E4M3X4)
+            turn_over(("d", q // 2), quarters(sorted_words["d", q, g]), doc_codes[q // 2, g][:, cols], doc_scale[q // 2, g][:, cols], E4M3X4)
 
         def rw_unit(i):
             codes = keep.tile([P, 2 * P], U32, name="rw_codes%d" % i, align_bytes=64)
             scales = keep.tile([P, 2 * P], U8, name="rw_scale%d" % i, align_bytes=64)
             rw_codes[i], rw_scale[i] = codes, scales
-            words = rw_sorted[i][:].bitcast(F32)
-            turn_over(("r", i), [words[:, slot * P : (slot + 1) * P] for slot in range(4)], BY_PASS, codes[:], scales[:], E5M2X4)
+            turn_over(("r", i), quarters(rw_sorted[i][:].bitcast(F32)), codes[:], scales[:], E5M2X4)
 
         def prior_unit(b):
             bank = new_bank()
             words = prior_rows[:].bitcast(F32)
             for c in range(4):
                 nc.tensor.transpose(bank[:, c * P : (c + 1) * P], words[:, 4 * b + c : 4 * b + c + 1].to_broadcast([P, P]), ident[:])
-            nc.vector.tensor_copy(
+            nc.scalar.copy(
                 out=prior_all[:].bitcast(F32).rearrange("m (p c) -> m p c", c=8)[:, :, 4 * b : 4 * b + 4],
                 in_=bank[:].rearrange("m (c p) -> m p c", c=4),
             )
 
         def delta_pass(bank, i, half, g):
-            for passes in HEAD + HALVES:
-                if g in passes:
-                    ensure(("c", i, passes))
+            for first in range(g + 1):
+                ensure(("c", i, first))
             nc.tensor.matmul_mx(
                 out=bank[:],
                 lhsT=ctx_codes[i, g].bitcast(E4M3X4),
@@ -207,22 +232,22 @@ def tile_query_rewrite_scoring_s9_kernel(tc, context, w_words, w_scales, turn, g
             cols = slice(half * BANK, (half + 1) * BANK)
             for u in range(2):
                 nc.vector.scalar_tensor_tensor(
-                    out=rw_sorted[i][:, cols].rearrange("p (u j e) -> p u j e", u=2, e=2)[:, u],
-                    in0=bank[:].rearrange("p (j u e) -> p u j e", u=2, e=2)[:, u],
+                    out=rw_sorted[i][:, cols].rearrange("p (u c i) -> p u c i", u=2, i=16)[:, u],
+                    in0=bank[:].rearrange("p (c u i) -> p u c i", u=2, i=16)[:, u],
                     scalar=gate_cols[:, i : i + 1],
-                    in1=turn_raw[i][:, cols].rearrange("p (j u e) -> p u j e", u=2, e=2)[:, u],
+                    in1=turn_raw[i][:, cols].rearrange("p (c u i) -> p u c i", u=2, i=16)[:, u],
                     op0=MULT,
                     op1=ADD,
                 )
 
-        def delta_unit(i, half):
+        def delta_unit(i, half, lead):
             bank = new_bank()
             for g in range(K_PASSES):
                 delta_pass(bank, i, half, g)
-            flush(QUANT_LAG)
+            quantise_pending(2 + lead)
             rewrite(bank, i, half)
 
-        def score_unit(i, j):
+        def score_unit(i, j, lead):
             ensure(("r", i))
             ensure(("d", j))
             bank = new_bank()
@@ -236,62 +261,79 @@ def tile_query_rewrite_scoring_s9_kernel(tc, context, w_words, w_scales, turn, g
                     start=(g == 0),
                     stop=(g == N_PASSES - 1),
                 )
-            flush(QUANT_LAG)
-            cols = slice(j * BANK, (j + 1) * BANK)
-            scores = work.tile([P, BANK], F32, name="scores", tag="scores", bufs=16)
-            nc.vector.tensor_tensor(out=scores[:], in0=bank[:], in1=prior_all[:, cols], op=ADD)
-            nc.sync.dma_start(out=out_rows[i][:, cols], in_=scores[:])
+            quantise_pending(lead)
+            parts = LAST_PARTS if len(scored) == M_TILES * D_CHUNKS else 1
+            width = BANK // parts
+            for part in range(parts):
+                cols = slice(j * BANK + part * width, j * BANK + (part + 1) * width)
+                scores = work.tile([P, width], F32, name="scores", tag="scores", bufs=16)
+                nc.vector.tensor_tensor(out=scores[:], in0=bank[:, part * width : (part + 1) * width], in1=prior_all[:, cols], op=ADD)
+                nc.sync.dma_start(out=out_rows[i][:, cols], in_=scores[:])
+            quantise_pending(1)
 
-        def sort_ctx(i):
-            if i < M_TILES and CTX_SORT[i]:
-                for passes in HALVES:
-                    sort_words(("c", i, passes), ctx_raw[i, passes][:], CTX_SORT[i])
-
-        def sort_docs(s):
-            for q in doc_steps[s]:
-                if DOC_SORT[q]:
-                    sort_words(("d", q), doc_raw[q][:], DOC_SORT[q])
-
-        prior_unit(0)
+        warm_up(WARM)
         ctx_unit(0, (0,))
-        flush(-1)
-        prior_unit(1)
-        for passes in HEAD[1:]:
-            ctx_unit(0, passes)
+        for b in range(EARLY):
+            prior_unit(b)
+        if SORT0:
+            sort_ctx(0, nc.vector.tensor_copy, HALVES[1:])
+        quantise_pending(1)
+        ctx_unit(0, (1,))
+        warm_up(WARM2)
+        ctx_unit(0, (2, 3))
         banks = [new_bank(), new_bank()]
-        for g in range(K_PASSES):
+        for g in HALVES[0]:
             for half in range(2):
                 delta_pass(banks[half], 0, half, g)
-        sort_ctx(1)
+        sort_ctx(1, nc.vector.tensor_copy)
+        quantise_pending(1)
+        for passes in HALVES:
+            ctx_unit(1, passes)
+        for b in range(EARLY, 2):
+            prior_unit(b)
+        for g in HALVES[1]:
+            for half in range(2):
+                delta_pass(banks[half], 0, half, g)
+        sort_ctx(2, nc.scalar.copy)
+        quantise_pending(2)
         for half in range(2):
             rewrite(banks[half], 0, half)
-        sort_docs(1)
 
         scored = []
+        turned = []
 
-        def score_some(count, tiles, chunks):
-            ready = [(i, j) for i in range(tiles) for j in range(chunks) if (i, j) not in scored]
-            for i, j in ready[:count]:
+        def ready_units():
+            return [(i, j) for i in rw_codes for j in range(len(turned) // 4) if (i, j) not in scored]
+
+        def score_some(units):
+            for i, j in units:
                 scored.append((i, j))
-                score_unit(i, j)
+                score_unit(i, j, 0)
 
-        for s in range(1, M_TILES + 1):
-            if s < M_TILES:
+        for s in range(1, M_TILES):
+            ready = ready_units()
+            delta_unit(s, 0, LEAD)
+            score_some(ready[: min(MID, (len(ready) + UP) // 2)])
+            if SORT_AT == 0:
+                sort_docs(s)
+            if s + 1 < M_TILES:
                 for passes in HALVES:
-                    ctx_unit(s, passes)
-            for q in doc_steps[s]:
-                doc_unit(q, 0)
-                doc_unit(q, 1)
+                    ctx_unit(s + 1, passes)
+            turned.extend(doc_steps[s - 1])
+            ready = ready_units()
             rw_unit(s - 1)
-            sort_ctx(s + 1)
-            score_some(BEFORE[s], s - 1, sum(DOC_PLAN[:s]) // 2)
-            if s < M_TILES:
-                if SORT_AT == 0:
-                    flush(QUANT_LAG - 1)
-                    sort_docs(s + 1)
-                delta_unit(s, 0)
-                if SORT_AT == 1:
-                    sort_docs(s + 1)
-                delta_unit(s, 1)
-            score_some(AFTER[s], s, sum(DOC_PLAN[: s + 1]) // 2)
+            if SORT_AT == 1:
+                sort_docs(s)
+            if s + 2 < M_TILES:
+                sort_ctx(s + 2, nc.scalar.copy if s > VS else nc.vector.tensor_copy)
+            delta_unit(s, 1, LEAD)
+            if s + 1 == M_TILES:
+                ready = ready_units()
+            score_some(ready[: min(MOST, len(ready) - HOLD if s + 1 == M_TILES else len(ready))])
+            for q, g in doc_steps[s]:
+                doc_unit(q, g)
+        ready = ready_units()
+        score_some(ready[:TAIL0])
+        rw_unit(M_TILES - 1)
+        score_some(ready_units())
         assert len(scored) == 32

@@ -26,24 +26,32 @@ D_GROUPS = D // 256
 D_CHUNKS = D // BANK
 
 EARLY = 1
+S2 = 1
+LATE = 7
+MERGE = 2
+LEAD0 = 2
+ON_S = 2
+GB = 6
+AFTER = 1
+DOC_LOAD = 0
 WARM = 0
 WARM2 = 0
 SORT0 = 1
 UP = 1
-SORT_AT = 0
-VS = 1
+SORT_AT = -1
+VS = 2
 TAIL0 = 0
-MID = 3
+MID = 4
 RUN = 3
 DOC_BANKS = 4
-DOC_FIRST = 1
+DOC_FIRST = 2
 HOLD = 3
-LEAD = 1
+LEAD = 3
 LAST_PARTS = 2
 HALVES = [(0, 1), (2, 3)]
 W_LOADS = [(0, 1), (2, 3)]
 DOC_SORT = "V"
-MOST = 4
+MOST = 5
 
 
 def tile_query_rewrite_scoring_s9_kernel(tc, context, w_words, w_scales, turn, gate, docs, prior, out):
@@ -111,20 +119,22 @@ def tile_query_rewrite_scoring_s9_kernel(tc, context, w_words, w_scales, turn, g
         rest = load("ctx0_rest", [P, K - BANK], BF16, context_rows[0][:, BANK:])
         load_w(W_LOADS[0])
         ctx_raw[0, (1,)], ctx_raw[0, (2, 3)] = rest[:, :BANK], rest[:, BANK:]
-        for q in range(4):
+        scale_rows = w_scales.rearrange("g (q r) n -> r q g n", r=4)
+        for r in range(4):
             nc.scalar.dma_start(
-                out=w_scale[32 * q : 32 * q + 4, :].bitcast(I32).rearrange("r (g n) -> r g n", g=K_PASSES),
-                in_=w_scales[:, 4 * q : 4 * q + 4, :].rearrange("g r n -> r g n").bitcast(I32),
+                out=w_scale[r:P:32, :].bitcast(I32).rearrange("q (g n) -> q g n", g=K_PASSES),
+                in_=scale_rows[r].bitcast(I32),
             )
         load_ctx(1)
         load_w(W_LOADS[1])
+        load_ctx(2)
         gate_cols = load("gate_cols", [P, M_TILES], BF16, gate.rearrange("(p i) -> p i", p=P))
         for s in range(M_TILES):
             turn_raw[s] = load("turn%d" % s, [P, N], BF16, turn_rows[s])
-            for q, g in doc_steps[s]:
+            for q, g in doc_steps[s + DOC_LOAD]:
                 if g == 0:
                     doc_raw[q] = load("docs%d" % q, [P, 2, N], BF16, doc_rows[q])
-            if s + 2 < M_TILES:
+            if 2 < s + 2 < M_TILES:
                 load_ctx(s + 2)
 
         prior_all = keep.tile([P, D], BF16, name="prior_all", align_bytes=64)
@@ -156,9 +166,8 @@ def tile_query_rewrite_scoring_s9_kernel(tc, context, w_words, w_scales, turn, g
                 )
                 sorted_words["c", i, passes] = tile
 
-        def sort_docs(s):
-            copy = nc.vector.tensor_copy if DOC_SORT == "V" else nc.scalar.copy
-            for q, g in doc_steps[s]:
+        def sort_docs(banks, copy):
+            for q, g in banks:
                 tile = work.tile([P, BANK], F32, name="doc_sorted", tag="doc_sorted", bufs=2 * DOC_BANKS)
                 copy(
                     out=tile[:].rearrange("p (a u c i) -> p a c u i", a=2, u=2, i=8),
@@ -167,15 +176,16 @@ def tile_query_rewrite_scoring_s9_kernel(tc, context, w_words, w_scales, turn, g
                 sorted_words["d", q, g] = tile
 
         def turn_over(key, sources, codes, scales, dtype):
-            bank = new_bank()
-            for slot, source in enumerate(sources):
-                nc.tensor.transpose(bank[:, slot * P : (slot + 1) * P], source, ident[:])
-            width = len(sources) * P
-            grouped = work.tile([P, 2 * width], BF16, name="grouped", tag="grouped", bufs=6, align_bytes=64)
-            nc.scalar.copy(
-                out=grouped[:].bitcast(F32).rearrange("p (a r u) -> p a r u", r=P, u=2),
-                in_=bank[:, :width].rearrange("p (a u r) -> p a r u", r=P, u=2),
-            )
+            grouped = work.tile([P, 2 * P * len(sources)], BF16, name="grouped", tag="grouped", bufs=GB, align_bytes=64)
+            for first in range(0, len(sources), 4):
+                part = sources[first : first + 4]
+                bank = new_bank()
+                for slot, source in enumerate(part):
+                    nc.tensor.transpose(bank[:, slot * P : (slot + 1) * P], source, ident[:])
+                nc.scalar.copy(
+                    out=grouped[:].bitcast(F32)[:, first * P : (first + len(part)) * P].rearrange("p (a r u) -> p a r u", r=P, u=2),
+                    in_=bank[:, : len(part) * P].rearrange("p (a u r) -> p a r u", r=P, u=2),
+                )
             pending.append((key, lambda: nc.vector.quantize_mx(out=codes.bitcast(dtype), scales=scales, in_=grouped[:])))
 
         def quarters(words):
@@ -186,16 +196,16 @@ def tile_query_rewrite_scoring_s9_kernel(tc, context, w_words, w_scales, turn, g
             scales = work.tile([P, len(passes) * P], U8, name="ctx_scale", tag="ctx_scale", bufs=6, align_bytes=64)
             for a, g in enumerate(passes):
                 ctx_codes[i, g], ctx_scale[i, g] = codes[:, a * P : (a + 1) * P], scales[:, a * P : (a + 1) * P]
-            if ("c", i, passes) not in sorted_words:
+            if ("c", i, passes[:2]) not in sorted_words:
                 words = ctx_raw[i, passes][:].bitcast(F32)
                 sources = [words[:, 2 * P * a + u : 2 * P * (a + 1) : 2] for a in range(len(passes)) for u in range(2)]
             else:
-                sources = quarters(sorted_words["c", i, passes])
+                sources = [s for h in range(0, len(passes), 2) for s in quarters(sorted_words["c", i, passes[h : h + 2]])]
             turn_over(("c", i, passes[0]), sources, codes[:], scales[:], E4M3X4)
 
-        def doc_unit(q, g):
-            cols = slice((q % 2) * 2 * P, (q % 2 + 1) * 2 * P)
-            turn_over(("d", q // 2), quarters(sorted_words["d", q, g]), doc_codes[q // 2, g][:, cols], doc_scale[q // 2, g][:, cols], E4M3X4)
+        def doc_unit(j, g):
+            sources = quarters(sorted_words["d", 2 * j, g]) + quarters(sorted_words["d", 2 * j + 1, g])
+            turn_over(("d", j), sources, doc_codes[j, g][:], doc_scale[j, g][:], E4M3X4)
 
         def rw_unit(i):
             codes = keep.tile([P, 2 * P], U32, name="rw_codes%d" % i, align_bytes=64)
@@ -244,7 +254,7 @@ def tile_query_rewrite_scoring_s9_kernel(tc, context, w_words, w_scales, turn, g
             bank = new_bank()
             for g in range(K_PASSES):
                 delta_pass(bank, i, half, g)
-            quantise_pending(2 + lead)
+            quantise_pending(lead)
             rewrite(bank, i, half)
 
         def score_unit(i, j, lead):
@@ -269,7 +279,7 @@ def tile_query_rewrite_scoring_s9_kernel(tc, context, w_words, w_scales, turn, g
                 scores = work.tile([P, width], F32, name="scores", tag="scores", bufs=16)
                 nc.vector.tensor_tensor(out=scores[:], in0=bank[:, part * width : (part + 1) * width], in1=prior_all[:, cols], op=ADD)
                 nc.sync.dma_start(out=out_rows[i][:, cols], in_=scores[:])
-            quantise_pending(1)
+            quantise_pending(AFTER)
 
         warm_up(WARM)
         ctx_unit(0, (0,))
@@ -289,12 +299,10 @@ def tile_query_rewrite_scoring_s9_kernel(tc, context, w_words, w_scales, turn, g
         quantise_pending(1)
         for passes in HALVES:
             ctx_unit(1, passes)
-        for b in range(EARLY, 2):
-            prior_unit(b)
         for g in HALVES[1]:
             for half in range(2):
                 delta_pass(banks[half], 0, half, g)
-        sort_ctx(2, nc.scalar.copy)
+        sort_ctx(2, nc.scalar.copy if S2 else nc.vector.tensor_copy)
         quantise_pending(2)
         for half in range(2):
             rewrite(banks[half], 0, half)
@@ -312,26 +320,36 @@ def tile_query_rewrite_scoring_s9_kernel(tc, context, w_words, w_scales, turn, g
 
         for s in range(1, M_TILES):
             ready = ready_units()
-            delta_unit(s, 0, LEAD)
+            if SORT_AT == -1:
+                sort_docs(doc_steps[s][ON_S:], nc.vector.tensor_copy)
+            delta_unit(s, 0, LEAD0)
             score_some(ready[: min(MID, (len(ready) + UP) // 2)])
             if SORT_AT == 0:
-                sort_docs(s)
+                sort_docs(doc_steps[s][ON_S:], nc.vector.tensor_copy)
             if s + 1 < M_TILES:
                 for passes in HALVES:
                     ctx_unit(s + 1, passes)
             turned.extend(doc_steps[s - 1])
             ready = ready_units()
             rw_unit(s - 1)
+            if s == 1:
+                for b in range(EARLY, 2):
+                    prior_unit(b)
+            for q, g in doc_steps[s][: 2 * MERGE : 2]:
+                doc_unit(q // 2, g)
+            if VS < s < M_TILES - 2:
+                sort_ctx(s + 2, nc.scalar.copy)
             if SORT_AT == 1:
-                sort_docs(s)
-            if s + 2 < M_TILES:
-                sort_ctx(s + 2, nc.scalar.copy if s > VS else nc.vector.tensor_copy)
+                sort_docs(doc_steps[s][ON_S:], nc.vector.tensor_copy)
             delta_unit(s, 1, LEAD)
-            if s + 1 == M_TILES:
+            if s <= VS:
+                sort_ctx(s + 2, nc.vector.tensor_copy)
+            if s >= LATE:
                 ready = ready_units()
             score_some(ready[: min(MOST, len(ready) - HOLD if s + 1 == M_TILES else len(ready))])
-            for q, g in doc_steps[s]:
-                doc_unit(q, g)
+            for q, g in doc_steps[s][2 * MERGE :: 2]:
+                doc_unit(q // 2, g)
+            sort_docs(doc_steps[s + 1][:ON_S], nc.scalar.copy)
         ready = ready_units()
         score_some(ready[:TAIL0])
         rw_unit(M_TILES - 1)

@@ -19,105 +19,74 @@ MULT = mybir.AluOpType.mult
 
 P = 128
 BANK = 512
+PSUM_BANKS = 8
+MX_ALIGN = 64
 M_TILES = M // P
 K_PASSES = K // BANK
 N_PASSES = N // BANK
-D_GROUPS = D // 256
 D_CHUNKS = D // BANK
+PASS_PAIRS = [(0, 1), (2, 3)]
+PIECES_PER_CHUNK = 4
 
-EARLY = 1
-S2 = 1
-LATE = 7
-MERGE = 2
-LEAD0 = 2
-ON_S = 2
-GB = 6
-AFTER = 1
-DOC_LOAD = 0
-WARM = 0
-WARM2 = 0
-SORT0 = 1
-UP = 1
-SORT_AT = -1
-VS = 2
-TAIL0 = 0
-MID = 4
-RUN = 3
-DOC_BANKS = 4
-DOC_FIRST = 2
-HOLD = 3
-LEAD = 3
-LAST_PARTS = 2
-HALVES = [(0, 1), (2, 3)]
-W_LOADS = [(0, 1), (2, 3)]
-DOC_SORT = "V"
-MOST = 5
+FIRST_DOC_STEP = 2
+LAST_CONTEXT_ON_VECTOR = 5
+DOC_PIECES_ON_SCALAR = 3
+HELD_BACK = 3
+LAST_STORES = 2
+
+SORTED_BUFS = 4
+GROUPED_BUFS = 6
+CONTEXT_CODE_BUFS = 6
+REWRITTEN_BUFS = 3
+SCORE_BUFS = 16
 
 
 def tile_query_rewrite_scoring_s9_kernel(tc, context, w_words, w_scales, turn, gate, docs, prior, out):
     nc = tc.nc
-    with ExitStack() as ctx:
-        keep = ctx.enter_context(tc.tile_pool(name="keep", bufs=1))
-        work = ctx.enter_context(tc.tile_pool(name="work", bufs=4))
-        psum = ctx.enter_context(tc.psum_pool(name="psum", bufs=8))
-        ctx.enter_context(tc.manual_schedule())
+    with ExitStack() as stack:
+        keep = stack.enter_context(tc.tile_pool(name="keep", bufs=1))
+        work = stack.enter_context(tc.tile_pool(name="work", bufs=SORTED_BUFS))
+        psum = stack.enter_context(tc.psum_pool(name="psum", bufs=PSUM_BANKS))
+        stack.enter_context(tc.manual_schedule())
 
         context_rows = context.rearrange("(p i) k -> i p k", i=M_TILES)
         turn_rows = turn.rearrange("(p i) n -> i p n", i=M_TILES)
         out_rows = out.rearrange("(p i) d -> i p d", i=M_TILES)
-        doc_rows = docs.rearrange("(q e p) n -> q p e n", p=P, e=2)
+        doc_rows = docs.rearrange("(q a p) n -> q p a n", p=P, a=2)
 
-        w_scale = keep.tile([P, K_PASSES * N], U8, name="w_scale", align_bytes=64)
+        w_scale = keep.tile([P, K_PASSES * N], U8, name="w_scale", align_bytes=MX_ALIGN)
         nc.vector.memset(w_scale[:].bitcast(I32), 0)
-        if WARM:
-            zeros = keep.tile([P, 864], U32, name="warm_zeros", align_bytes=64)
-            nc.vector.memset(zeros[:], 0)
-            moving, moving_scale = zeros[:, :512], zeros[:, 512:640].bitcast(U8)
-            fixed, fixed_scale = zeros[:, 640:768], zeros[:, 768:800].bitcast(U8)
-            source = zeros[:, 800:864].bitcast(BF16)
-            nc.vector.quantize_mx(out=moving[:, :32].bitcast(E4M3X4), scales=moving_scale[:, :32], in_=source)
-            nc.vector.quantize_mx(out=fixed[:, :32].bitcast(E5M2X4), scales=fixed_scale[:, :32], in_=source)
-
-        def warm_up(count):
-            if count:
-                bank = new_bank()
-            for n in range(count):
-                nc.tensor.matmul_mx(
-                    out=bank[:], lhsT=fixed.bitcast(E5M2X4), lhsT_scale=fixed_scale, rhs=moving.bitcast(E4M3X4), rhs_scale=moving_scale,
-                    start=(n == 0), stop=(n == count - 1),
-                )
-
         ident = keep.tile([P, P], F32, name="ident")
         make_identity(nc, ident[:])
 
-        def load(name, shape, dtype, source, queue=nc.sync):
-            tile = keep.tile(shape, dtype, name=name, align_bytes=64)
+        ctx_raw, turn_raw, doc_raw, w_codes = {}, {}, {}, {}
+
+        def load(name, shape, source, queue=nc.sync):
+            tile = keep.tile(shape, BF16, name=name, align_bytes=MX_ALIGN)
             queue.dma_start(out=tile[:], in_=source)
             return tile
 
         def load_w(passes):
             first, count = passes[0], len(passes)
-            tile = keep.tile([P, count, 2 * N], U8, name="w_codes%d" % first, align_bytes=64)
+            tile = keep.tile([P, count, 2 * N], U8, name="w_codes%d" % first, align_bytes=MX_ALIGN)
             source = w_words[first : first + count].rearrange("g p b -> p g b")
             nc.sync.dma_start(out=tile[:].bitcast(I32), in_=source.bitcast(I32))
             for g in passes:
                 w_codes[g] = tile[:, g - first, :]
 
-        def load_ctx(i):
-            tile = load("ctx%d" % i, [P, K], BF16, context_rows[i])
-            for passes in HALVES:
+        def load_context(i):
+            tile = load("ctx%d" % i, [P, K], context_rows[i])
+            for passes in PASS_PAIRS:
                 ctx_raw[i, passes] = tile[:, BANK * passes[0] : BANK * (passes[-1] + 1)]
 
-        doc_banks = [(2 * j + e, g) for j in range(D_CHUNKS) for g in range(N_PASSES) for e in range(2)]
-        doc_steps = {s: [] for s in range(M_TILES + 2)}
-        for n, bank_id in enumerate(doc_banks):
-            doc_steps[DOC_FIRST + n // DOC_BANKS].append(bank_id)
+        def doc_pieces(s):
+            j = s - FIRST_DOC_STEP
+            return [(2 * j + a, g) for g in range(N_PASSES) for a in range(2)] if 0 <= j < D_CHUNKS else []
 
-        ctx_raw, turn_raw, doc_raw, w_codes = {}, {}, {}, {}
-        ctx_raw[0, (0,)] = load("ctx0_first", [P, BANK], BF16, context_rows[0][:, :BANK])
-        prior_rows = load("prior_rows", [P, D // P], BF16, prior.rearrange("(p c) -> p c", p=P), nc.scalar)
-        rest = load("ctx0_rest", [P, K - BANK], BF16, context_rows[0][:, BANK:])
-        load_w(W_LOADS[0])
+        ctx_raw[0, (0,)] = load("ctx0_first", [P, BANK], context_rows[0][:, :BANK])
+        prior_rows = load("prior_rows", [P, D // P], prior.rearrange("(p c) -> p c", p=P), nc.scalar)
+        rest = load("ctx0_rest", [P, K - BANK], context_rows[0][:, BANK:])
+        load_w(PASS_PAIRS[0])
         ctx_raw[0, (1,)], ctx_raw[0, (2, 3)] = rest[:, :BANK], rest[:, BANK:]
         scale_rows = w_scales.rearrange("g (q r) n -> r q g n", r=4)
         for r in range(4):
@@ -125,107 +94,114 @@ def tile_query_rewrite_scoring_s9_kernel(tc, context, w_words, w_scales, turn, g
                 out=w_scale[r:P:32, :].bitcast(I32).rearrange("q (g n) -> q g n", g=K_PASSES),
                 in_=scale_rows[r].bitcast(I32),
             )
-        load_ctx(1)
-        load_w(W_LOADS[1])
-        load_ctx(2)
-        gate_cols = load("gate_cols", [P, M_TILES], BF16, gate.rearrange("(p i) -> p i", p=P))
+        load_context(1)
+        load_w(PASS_PAIRS[1])
+        load_context(2)
+        gate_cols = load("gate_cols", [P, M_TILES], gate.rearrange("(p i) -> p i", p=P))
         for s in range(M_TILES):
-            turn_raw[s] = load("turn%d" % s, [P, N], BF16, turn_rows[s])
-            for q, g in doc_steps[s + DOC_LOAD]:
+            turn_raw[s] = load("turn%d" % s, [P, N], turn_rows[s])
+            for q, g in doc_pieces(s):
                 if g == 0:
-                    doc_raw[q] = load("docs%d" % q, [P, 2, N], BF16, doc_rows[q])
+                    doc_raw[q] = load("docs%d" % q, [P, 2, N], doc_rows[q])
             if 2 < s + 2 < M_TILES:
-                load_ctx(s + 2)
+                load_context(s + 2)
 
-        prior_all = keep.tile([P, D], BF16, name="prior_all", align_bytes=64)
+        prior_all = keep.tile([P, D], BF16, name="prior_all", align_bytes=MX_ALIGN)
         doc_codes, doc_scale = {}, {}
         for j in range(D_CHUNKS):
             for g in range(N_PASSES):
-                doc_codes[j, g] = keep.tile([P, BANK], U32, name="doc_codes%d_%d" % (j, g), align_bytes=64)
-                doc_scale[j, g] = keep.tile([P, BANK], U8, name="doc_scale%d_%d" % (j, g), align_bytes=64)
-        ctx_codes, ctx_scale, rw_codes, rw_scale, rw_sorted, sorted_words = {}, {}, {}, {}, {}, {}
-        pending = []
+                doc_codes[j, g] = keep.tile([P, BANK], U32, name="doc_codes%d_%d" % (j, g), align_bytes=MX_ALIGN)
+                doc_scale[j, g] = keep.tile([P, BANK], U8, name="doc_scale%d_%d" % (j, g), align_bytes=MX_ALIGN)
+        ctx_codes, ctx_scale, rw_codes, rw_scale, rw_sorted, ctx_sorted, doc_sorted = {}, {}, {}, {}, {}, {}, {}
 
-        def new_bank():
-            return psum.tile([P, BANK], F32, name="bank")
+        pending = []
 
         def quantise_pending(count):
             for n in range(min(count, len(pending))):
                 pending.pop(0)[1]()
 
-        def ensure(key):
+        def quantise_up_to(key):
             while any(entry[0] == key for entry in pending):
                 quantise_pending(1)
 
-        def sort_ctx(i, copy, parts=HALVES):
-            for passes in parts:
+        def new_bank():
+            return psum.tile([P, BANK], F32, name="bank")
+
+        def sort_context(i, copy, pairs=PASS_PAIRS):
+            for passes in pairs:
                 tile = work.tile([P, BANK], F32, name="ctx_sorted", tag="ctx_sorted")
                 copy(
                     out=tile[:].rearrange("p (a u c i) -> p a c u i", a=2, u=2, i=4),
                     in_=ctx_raw[i, passes].bitcast(F32).rearrange("p (a c i u) -> p a c u i", a=2, u=2, i=4),
                 )
-                sorted_words["c", i, passes] = tile
+                ctx_sorted[i, passes] = tile
 
-        def sort_docs(banks, copy):
-            for q, g in banks:
-                tile = work.tile([P, BANK], F32, name="doc_sorted", tag="doc_sorted", bufs=2 * DOC_BANKS)
+        def sort_docs(pieces, copy):
+            for q, g in pieces:
+                tile = work.tile([P, BANK], F32, name="doc_sorted", tag="doc_sorted", bufs=2 * PIECES_PER_CHUNK)
+                words = doc_raw[q][:, :, BANK * g : BANK * (g + 1)].bitcast(F32)
                 copy(
-                    out=tile[:].rearrange("p (a u c i) -> p a c u i", a=2, u=2, i=8),
-                    in_=doc_raw[q][:, :, BANK * g : BANK * (g + 1)].bitcast(F32).rearrange("p a (c u i) -> p a c u i", u=2, i=8),
+                    out=tile[:].rearrange("p (a u b r) -> p a b u r", a=2, u=2, r=8),
+                    in_=words.rearrange("p a (b u r) -> p a b u r", u=2, r=8),
                 )
-                sorted_words["d", q, g] = tile
+                doc_sorted[q, g] = tile
 
         def turn_over(key, sources, codes, scales, dtype):
-            grouped = work.tile([P, 2 * P * len(sources)], BF16, name="grouped", tag="grouped", bufs=GB, align_bytes=64)
+            grouped = work.tile(
+                [P, 2 * P * len(sources)], BF16, name="grouped", tag="grouped", bufs=GROUPED_BUFS, align_bytes=MX_ALIGN
+            )
             for first in range(0, len(sources), 4):
                 part = sources[first : first + 4]
                 bank = new_bank()
                 for slot, source in enumerate(part):
                     nc.tensor.transpose(bank[:, slot * P : (slot + 1) * P], source, ident[:])
+                target = grouped[:].bitcast(F32)[:, first * P : (first + len(part)) * P]
                 nc.scalar.copy(
-                    out=grouped[:].bitcast(F32)[:, first * P : (first + len(part)) * P].rearrange("p (a r u) -> p a r u", r=P, u=2),
-                    in_=bank[:, : len(part) * P].rearrange("p (a u r) -> p a r u", r=P, u=2),
+                    out=target.rearrange("p (a row u) -> p a row u", row=P, u=2),
+                    in_=bank[:, : len(part) * P].rearrange("p (a u row) -> p a row u", row=P, u=2),
                 )
             pending.append((key, lambda: nc.vector.quantize_mx(out=codes.bitcast(dtype), scales=scales, in_=grouped[:])))
 
         def quarters(words):
             return [words[:, slot * P : (slot + 1) * P] for slot in range(4)]
 
-        def ctx_unit(i, passes):
-            codes = work.tile([P, len(passes) * P], U32, name="ctx_codes", tag="ctx_codes", bufs=6, align_bytes=64)
-            scales = work.tile([P, len(passes) * P], U8, name="ctx_scale", tag="ctx_scale", bufs=6, align_bytes=64)
+        def turn_context(i, passes):
+            width = len(passes) * P
+            codes = work.tile([P, width], U32, name="ctx_codes", tag="ctx_codes", bufs=CONTEXT_CODE_BUFS, align_bytes=MX_ALIGN)
+            scales = work.tile([P, width], U8, name="ctx_scale", tag="ctx_scale", bufs=CONTEXT_CODE_BUFS, align_bytes=MX_ALIGN)
             for a, g in enumerate(passes):
                 ctx_codes[i, g], ctx_scale[i, g] = codes[:, a * P : (a + 1) * P], scales[:, a * P : (a + 1) * P]
-            if ("c", i, passes[:2]) not in sorted_words:
+            if (i, passes) in ctx_sorted:
+                sources = quarters(ctx_sorted[i, passes])
+            else:
                 words = ctx_raw[i, passes][:].bitcast(F32)
                 sources = [words[:, 2 * P * a + u : 2 * P * (a + 1) : 2] for a in range(len(passes)) for u in range(2)]
-            else:
-                sources = [s for h in range(0, len(passes), 2) for s in quarters(sorted_words["c", i, passes[h : h + 2]])]
-            turn_over(("c", i, passes[0]), sources, codes[:], scales[:], E4M3X4)
+            turn_over(("context", i, passes[0]), sources, codes[:], scales[:], E4M3X4)
 
-        def doc_unit(j, g):
-            sources = quarters(sorted_words["d", 2 * j, g]) + quarters(sorted_words["d", 2 * j + 1, g])
-            turn_over(("d", j), sources, doc_codes[j, g][:], doc_scale[j, g][:], E4M3X4)
+        def turn_docs(j, g):
+            sources = quarters(doc_sorted[2 * j, g]) + quarters(doc_sorted[2 * j + 1, g])
+            turn_over(("docs", j), sources, doc_codes[j, g][:], doc_scale[j, g][:], E4M3X4)
 
-        def rw_unit(i):
-            codes = keep.tile([P, 2 * P], U32, name="rw_codes%d" % i, align_bytes=64)
-            scales = keep.tile([P, 2 * P], U8, name="rw_scale%d" % i, align_bytes=64)
-            rw_codes[i], rw_scale[i] = codes, scales
-            turn_over(("r", i), quarters(rw_sorted[i][:].bitcast(F32)), codes[:], scales[:], E5M2X4)
+        def turn_rewritten(i):
+            rw_codes[i] = keep.tile([P, N_PASSES * P], U32, name="rw_codes%d" % i, align_bytes=MX_ALIGN)
+            rw_scale[i] = keep.tile([P, N_PASSES * P], U8, name="rw_scale%d" % i, align_bytes=MX_ALIGN)
+            sources = quarters(rw_sorted[i][:].bitcast(F32))
+            turn_over(("rewritten", i), sources, rw_codes[i][:], rw_scale[i][:], E5M2X4)
 
-        def prior_unit(b):
+        def spread_prior(part):
             bank = new_bank()
             words = prior_rows[:].bitcast(F32)
             for c in range(4):
-                nc.tensor.transpose(bank[:, c * P : (c + 1) * P], words[:, 4 * b + c : 4 * b + c + 1].to_broadcast([P, P]), ident[:])
+                column = words[:, 4 * part + c : 4 * part + c + 1]
+                nc.tensor.transpose(bank[:, c * P : (c + 1) * P], column.to_broadcast([P, P]), ident[:])
             nc.scalar.copy(
-                out=prior_all[:].bitcast(F32).rearrange("m (p c) -> m p c", c=8)[:, :, 4 * b : 4 * b + 4],
+                out=prior_all[:].bitcast(F32).rearrange("m (p c) -> m p c", c=8)[:, :, 4 * part : 4 * part + 4],
                 in_=bank[:].rearrange("m (c p) -> m p c", c=4),
             )
 
         def delta_pass(bank, i, half, g):
             for first in range(g + 1):
-                ensure(("c", i, first))
+                quantise_up_to(("context", i, first))
             nc.tensor.matmul_mx(
                 out=bank[:],
                 lhsT=ctx_codes[i, g].bitcast(E4M3X4),
@@ -236,122 +212,115 @@ def tile_query_rewrite_scoring_s9_kernel(tc, context, w_words, w_scales, turn, g
                 stop=(g == K_PASSES - 1),
             )
 
+        def delta_half(i, half):
+            bank = new_bank()
+            for g in range(K_PASSES):
+                delta_pass(bank, i, half, g)
+            return bank
+
         def rewrite(bank, i, half):
             if half == 0:
-                rw_sorted[i] = work.tile([P, N], BF16, name="rw_sorted", tag="rw_sorted", bufs=3)
+                rw_sorted[i] = work.tile([P, N], BF16, name="rw_sorted", tag="rw_sorted", bufs=REWRITTEN_BUFS)
             cols = slice(half * BANK, (half + 1) * BANK)
             for u in range(2):
                 nc.vector.scalar_tensor_tensor(
-                    out=rw_sorted[i][:, cols].rearrange("p (u c i) -> p u c i", u=2, i=16)[:, u],
-                    in0=bank[:].rearrange("p (c u i) -> p u c i", u=2, i=16)[:, u],
+                    out=rw_sorted[i][:, cols].rearrange("p (u b x) -> p u b x", u=2, x=16)[:, u],
+                    in0=bank[:].rearrange("p (b u x) -> p u b x", u=2, x=16)[:, u],
                     scalar=gate_cols[:, i : i + 1],
-                    in1=turn_raw[i][:, cols].rearrange("p (c u i) -> p u c i", u=2, i=16)[:, u],
+                    in1=turn_raw[i][:, cols].rearrange("p (b u x) -> p u b x", u=2, x=16)[:, u],
                     op0=MULT,
                     op1=ADD,
                 )
 
-        def delta_unit(i, half, lead):
-            bank = new_bank()
-            for g in range(K_PASSES):
-                delta_pass(bank, i, half, g)
-            quantise_pending(lead)
-            rewrite(bank, i, half)
+        scored = []
 
-        def score_unit(i, j, lead):
-            ensure(("r", i))
-            ensure(("d", j))
-            bank = new_bank()
-            for g in range(N_PASSES):
-                nc.tensor.matmul_mx(
-                    out=bank[:],
-                    lhsT=rw_codes[i][:, g * P : (g + 1) * P].bitcast(E5M2X4),
-                    lhsT_scale=rw_scale[i][:, g * P : (g + 1) * P],
-                    rhs=doc_codes[j, g][:].bitcast(E4M3X4),
-                    rhs_scale=doc_scale[j, g][:],
-                    start=(g == 0),
-                    stop=(g == N_PASSES - 1),
-                )
-            quantise_pending(lead)
-            parts = LAST_PARTS if len(scored) == M_TILES * D_CHUNKS else 1
-            width = BANK // parts
-            for part in range(parts):
-                cols = slice(j * BANK + part * width, j * BANK + (part + 1) * width)
-                scores = work.tile([P, width], F32, name="scores", tag="scores", bufs=16)
-                nc.vector.tensor_tensor(out=scores[:], in0=bank[:, part * width : (part + 1) * width], in1=prior_all[:, cols], op=ADD)
-                nc.sync.dma_start(out=out_rows[i][:, cols], in_=scores[:])
-            quantise_pending(AFTER)
+        def score(patches):
+            for i, j in patches:
+                scored.append((i, j))
+                quantise_up_to(("rewritten", i))
+                quantise_up_to(("docs", j))
+                bank = new_bank()
+                for g in range(N_PASSES):
+                    nc.tensor.matmul_mx(
+                        out=bank[:],
+                        lhsT=rw_codes[i][:, g * P : (g + 1) * P].bitcast(E5M2X4),
+                        lhsT_scale=rw_scale[i][:, g * P : (g + 1) * P],
+                        rhs=doc_codes[j, g][:].bitcast(E4M3X4),
+                        rhs_scale=doc_scale[j, g][:],
+                        start=(g == 0),
+                        stop=(g == N_PASSES - 1),
+                    )
+                parts = LAST_STORES if len(scored) == M_TILES * D_CHUNKS else 1
+                width = BANK // parts
+                for part in range(parts):
+                    cols = slice(j * BANK + part * width, j * BANK + (part + 1) * width)
+                    scores = work.tile([P, width], F32, name="scores", tag="scores", bufs=SCORE_BUFS)
+                    nc.vector.tensor_tensor(
+                        out=scores[:], in0=bank[:, part * width : (part + 1) * width], in1=prior_all[:, cols], op=ADD
+                    )
+                    nc.sync.dma_start(out=out_rows[i][:, cols], in_=scores[:])
+                quantise_pending(1)
 
-        warm_up(WARM)
-        ctx_unit(0, (0,))
-        for b in range(EARLY):
-            prior_unit(b)
-        if SORT0:
-            sort_ctx(0, nc.vector.tensor_copy, HALVES[1:])
+        def open_patches(tiles, last_doc_step):
+            chunks = min(last_doc_step - FIRST_DOC_STEP + 1, D_CHUNKS)
+            return [(i, j) for i in range(tiles) for j in range(chunks) if (i, j) not in scored]
+
+        def pieces_on_scalar(s):
+            return DOC_PIECES_ON_SCALAR if s > FIRST_DOC_STEP else 0
+
+        turn_context(0, (0,))
+        spread_prior(0)
+        sort_context(0, nc.vector.tensor_copy, PASS_PAIRS[1:])
         quantise_pending(1)
-        ctx_unit(0, (1,))
-        warm_up(WARM2)
-        ctx_unit(0, (2, 3))
+        turn_context(0, (1,))
+        turn_context(0, (2, 3))
         banks = [new_bank(), new_bank()]
-        for g in HALVES[0]:
+        for g in PASS_PAIRS[0]:
             for half in range(2):
                 delta_pass(banks[half], 0, half, g)
-        sort_ctx(1, nc.vector.tensor_copy)
         quantise_pending(1)
-        for passes in HALVES:
-            ctx_unit(1, passes)
-        for g in HALVES[1]:
+        for passes in PASS_PAIRS:
+            turn_context(1, passes)
+        for g in PASS_PAIRS[1]:
             for half in range(2):
                 delta_pass(banks[half], 0, half, g)
-        sort_ctx(2, nc.scalar.copy if S2 else nc.vector.tensor_copy)
+        sort_context(2, nc.scalar.copy)
         quantise_pending(2)
         for half in range(2):
             rewrite(banks[half], 0, half)
 
-        scored = []
-        turned = []
-
-        def ready_units():
-            return [(i, j) for i in rw_codes for j in range(len(turned) // 4) if (i, j) not in scored]
-
-        def score_some(units):
-            for i, j in units:
-                scored.append((i, j))
-                score_unit(i, j, 0)
-
         for s in range(1, M_TILES):
-            ready = ready_units()
-            if SORT_AT == -1:
-                sort_docs(doc_steps[s][ON_S:], nc.vector.tensor_copy)
-            delta_unit(s, 0, LEAD0)
-            score_some(ready[: min(MID, (len(ready) + UP) // 2)])
-            if SORT_AT == 0:
-                sort_docs(doc_steps[s][ON_S:], nc.vector.tensor_copy)
-            if s + 1 < M_TILES:
-                for passes in HALVES:
-                    ctx_unit(s + 1, passes)
-            turned.extend(doc_steps[s - 1])
-            ready = ready_units()
-            rw_unit(s - 1)
+            last = s + 1 == M_TILES
+            sort_docs(doc_pieces(s)[pieces_on_scalar(s) :], nc.vector.tensor_copy)
+            bank = delta_half(s, 0)
+            quantise_pending(N_PASSES)
+            rewrite(bank, s, 0)
+            patches = open_patches(s - 1, s - 2)
+            score(patches[: (len(patches) + 1) // 2])
+
+            if not last:
+                for passes in PASS_PAIRS:
+                    turn_context(s + 1, passes)
+            turn_rewritten(s - 1)
             if s == 1:
-                for b in range(EARLY, 2):
-                    prior_unit(b)
-            for q, g in doc_steps[s][: 2 * MERGE : 2]:
-                doc_unit(q // 2, g)
-            if VS < s < M_TILES - 2:
-                sort_ctx(s + 2, nc.scalar.copy)
-            if SORT_AT == 1:
-                sort_docs(doc_steps[s][ON_S:], nc.vector.tensor_copy)
-            delta_unit(s, 1, LEAD)
-            if s <= VS:
-                sort_ctx(s + 2, nc.vector.tensor_copy)
-            if s >= LATE:
-                ready = ready_units()
-            score_some(ready[: min(MOST, len(ready) - HOLD if s + 1 == M_TILES else len(ready))])
-            for q, g in doc_steps[s][2 * MERGE :: 2]:
-                doc_unit(q // 2, g)
-            sort_docs(doc_steps[s + 1][:ON_S], nc.scalar.copy)
-        ready = ready_units()
-        score_some(ready[:TAIL0])
-        rw_unit(M_TILES - 1)
-        score_some(ready_units())
-        assert len(scored) == 32
+                spread_prior(1)
+            if doc_pieces(s):
+                for g in range(N_PASSES):
+                    turn_docs(s - FIRST_DOC_STEP, g)
+            if LAST_CONTEXT_ON_VECTOR < s + 2 < M_TILES:
+                sort_context(s + 2, nc.scalar.copy)
+
+            bank = delta_half(s, 1)
+            quantise_pending(len(PASS_PAIRS))
+            if s + 2 <= LAST_CONTEXT_ON_VECTOR:
+                sort_context(s + 2, nc.vector.tensor_copy)
+            quantise_pending(1)
+            rewrite(bank, s, 1)
+            if last:
+                score(open_patches(s, s)[:-HELD_BACK])
+            else:
+                score(open_patches(s - 1, s - 1))
+            sort_docs(doc_pieces(s + 1)[: pieces_on_scalar(s + 1)], nc.scalar.copy)
+
+        turn_rewritten(M_TILES - 1)
+        score(open_patches(M_TILES, M_TILES))

from contextlib import ExitStack

import concourse.mybir as mybir
from concourse.masks import make_identity

M, K, N, D = 1024, 2048, 1024, 2048
FLOPS = 2 * M * K * N + 2 * M * N * D

F32 = mybir.dt.float32
BF16 = mybir.dt.bfloat16
I32 = mybir.dt.int32
U32 = mybir.dt.uint32
U8 = mybir.dt.uint8
E4M3X4 = mybir.dt.float8_e4m3fn_x4
E5M2X4 = mybir.dt.float8_e5m2_x4
E2M1X4 = mybir.dt.float4_e2m1fn_x4
ADD = mybir.AluOpType.add
MULT = mybir.AluOpType.mult

P = 128
BANK = 512
PSUM_BANKS = 8
MX_ALIGN = 64
M_TILES = M // P
K_PASSES = K // BANK
N_PASSES = N // BANK
D_CHUNKS = D // BANK
PASS_PAIRS = [(0, 1), (2, 3)]
PIECES_PER_CHUNK = 4

FIRST_DOC_STEP = 2
LAST_CONTEXT_ON_VECTOR = 5
DOC_PIECES_ON_SCALAR = 3
HELD_BACK = 3
LAST_STORES = 2

SORTED_BUFS = 4
GROUPED_BUFS = 6
CONTEXT_CODE_BUFS = 6
REWRITTEN_BUFS = 3
SCORE_BUFS = 16


def tile_query_rewrite_scoring_s9_kernel(tc, context, w_words, w_scales, turn, gate, docs, prior, out):
    nc = tc.nc
    with ExitStack() as stack:
        keep = stack.enter_context(tc.tile_pool(name="keep", bufs=1))
        work = stack.enter_context(tc.tile_pool(name="work", bufs=SORTED_BUFS))
        psum = stack.enter_context(tc.psum_pool(name="psum", bufs=PSUM_BANKS))
        stack.enter_context(tc.manual_schedule())

        context_rows = context.rearrange("(p i) k -> i p k", i=M_TILES)
        turn_rows = turn.rearrange("(p i) n -> i p n", i=M_TILES)
        out_rows = out.rearrange("(p i) d -> i p d", i=M_TILES)
        doc_rows = docs.rearrange("(q a p) n -> q p a n", p=P, a=2)

        w_scale = keep.tile([P, K_PASSES * N], U8, name="w_scale", align_bytes=MX_ALIGN)
        nc.vector.memset(w_scale[:].bitcast(I32), 0)
        ident = keep.tile([P, P], F32, name="ident")
        make_identity(nc, ident[:])

        ctx_raw, turn_raw, doc_raw, w_codes = {}, {}, {}, {}

        def load(name, shape, source, queue=nc.sync):
            tile = keep.tile(shape, BF16, name=name, align_bytes=MX_ALIGN)
            queue.dma_start(out=tile[:], in_=source)
            return tile

        def load_w(passes):
            first, count = passes[0], len(passes)
            tile = keep.tile([P, count, 2 * N], U8, name="w_codes%d" % first, align_bytes=MX_ALIGN)
            source = w_words[first : first + count].rearrange("g p b -> p g b")
            nc.sync.dma_start(out=tile[:].bitcast(I32), in_=source.bitcast(I32))
            for g in passes:
                w_codes[g] = tile[:, g - first, :]

        def load_context(i):
            tile = load("ctx%d" % i, [P, K], context_rows[i])
            for passes in PASS_PAIRS:
                ctx_raw[i, passes] = tile[:, BANK * passes[0] : BANK * (passes[-1] + 1)]

        def doc_pieces(s):
            j = s - FIRST_DOC_STEP
            return [(2 * j + a, g) for g in range(N_PASSES) for a in range(2)] if 0 <= j < D_CHUNKS else []

        ctx_raw[0, (0,)] = load("ctx0_first", [P, BANK], context_rows[0][:, :BANK])
        prior_rows = load("prior_rows", [P, D // P], prior.rearrange("(p c) -> p c", p=P), nc.scalar)
        rest = load("ctx0_rest", [P, K - BANK], context_rows[0][:, BANK:])
        load_w(PASS_PAIRS[0])
        ctx_raw[0, (1,)], ctx_raw[0, (2, 3)] = rest[:, :BANK], rest[:, BANK:]
        scale_rows = w_scales.rearrange("g (q r) n -> r q g n", r=4)
        for r in range(4):
            nc.scalar.dma_start(
                out=w_scale[r:P:32, :].bitcast(I32).rearrange("q (g n) -> q g n", g=K_PASSES),
                in_=scale_rows[r].bitcast(I32),
            )
        load_context(1)
        load_w(PASS_PAIRS[1])
        load_context(2)
        gate_cols = load("gate_cols", [P, M_TILES], gate.rearrange("(p i) -> p i", p=P))
        for s in range(M_TILES):
            turn_raw[s] = load("turn%d" % s, [P, N], turn_rows[s])
            for q, g in doc_pieces(s):
                if g == 0:
                    doc_raw[q] = load("docs%d" % q, [P, 2, N], doc_rows[q])
            if 2 < s + 2 < M_TILES:
                load_context(s + 2)

        prior_all = keep.tile([P, D], BF16, name="prior_all", align_bytes=MX_ALIGN)
        doc_codes, doc_scale = {}, {}
        for j in range(D_CHUNKS):
            for g in range(N_PASSES):
                doc_codes[j, g] = keep.tile([P, BANK], U32, name="doc_codes%d_%d" % (j, g), align_bytes=MX_ALIGN)
                doc_scale[j, g] = keep.tile([P, BANK], U8, name="doc_scale%d_%d" % (j, g), align_bytes=MX_ALIGN)
        ctx_codes, ctx_scale, rw_codes, rw_scale, rw_sorted, ctx_sorted, doc_sorted = {}, {}, {}, {}, {}, {}, {}

        pending = []

        def quantise_pending(count):
            for n in range(min(count, len(pending))):
                pending.pop(0)[1]()

        def quantise_up_to(key):
            while any(entry[0] == key for entry in pending):
                quantise_pending(1)

        def new_bank():
            return psum.tile([P, BANK], F32, name="bank")

        def sort_context(i, copy, pairs=PASS_PAIRS):
            for passes in pairs:
                tile = work.tile([P, BANK], F32, name="ctx_sorted", tag="ctx_sorted")
                copy(
                    out=tile[:].rearrange("p (a u c i) -> p a c u i", a=2, u=2, i=4),
                    in_=ctx_raw[i, passes].bitcast(F32).rearrange("p (a c i u) -> p a c u i", a=2, u=2, i=4),
                )
                ctx_sorted[i, passes] = tile

        def sort_docs(pieces, copy):
            for q, g in pieces:
                tile = work.tile([P, BANK], F32, name="doc_sorted", tag="doc_sorted", bufs=2 * PIECES_PER_CHUNK)
                words = doc_raw[q][:, :, BANK * g : BANK * (g + 1)].bitcast(F32)
                copy(
                    out=tile[:].rearrange("p (a u b r) -> p a b u r", a=2, u=2, r=8),
                    in_=words.rearrange("p a (b u r) -> p a b u r", u=2, r=8),
                )
                doc_sorted[q, g] = tile

        def turn_over(key, sources, codes, scales, dtype):
            grouped = work.tile(
                [P, 2 * P * len(sources)], BF16, name="grouped", tag="grouped", bufs=GROUPED_BUFS, align_bytes=MX_ALIGN
            )
            for first in range(0, len(sources), 4):
                part = sources[first : first + 4]
                bank = new_bank()
                for slot, source in enumerate(part):
                    nc.tensor.transpose(bank[:, slot * P : (slot + 1) * P], source, ident[:])
                target = grouped[:].bitcast(F32)[:, first * P : (first + len(part)) * P]
                nc.scalar.copy(
                    out=target.rearrange("p (a row u) -> p a row u", row=P, u=2),
                    in_=bank[:, : len(part) * P].rearrange("p (a u row) -> p a row u", row=P, u=2),
                )
            pending.append((key, lambda: nc.vector.quantize_mx(out=codes.bitcast(dtype), scales=scales, in_=grouped[:])))

        def quarters(words):
            return [words[:, slot * P : (slot + 1) * P] for slot in range(4)]

        def turn_context(i, passes):
            width = len(passes) * P
            codes = work.tile([P, width], U32, name="ctx_codes", tag="ctx_codes", bufs=CONTEXT_CODE_BUFS, align_bytes=MX_ALIGN)
            scales = work.tile([P, width], U8, name="ctx_scale", tag="ctx_scale", bufs=CONTEXT_CODE_BUFS, align_bytes=MX_ALIGN)
            for a, g in enumerate(passes):
                ctx_codes[i, g], ctx_scale[i, g] = codes[:, a * P : (a + 1) * P], scales[:, a * P : (a + 1) * P]
            if (i, passes) in ctx_sorted:
                sources = quarters(ctx_sorted[i, passes])
            else:
                words = ctx_raw[i, passes][:].bitcast(F32)
                sources = [words[:, 2 * P * a + u : 2 * P * (a + 1) : 2] for a in range(len(passes)) for u in range(2)]
            turn_over(("context", i, passes[0]), sources, codes[:], scales[:], E4M3X4)

        def turn_docs(j, g):
            sources = quarters(doc_sorted[2 * j, g]) + quarters(doc_sorted[2 * j + 1, g])
            turn_over(("docs", j), sources, doc_codes[j, g][:], doc_scale[j, g][:], E4M3X4)

        def turn_rewritten(i):
            rw_codes[i] = keep.tile([P, N_PASSES * P], U32, name="rw_codes%d" % i, align_bytes=MX_ALIGN)
            rw_scale[i] = keep.tile([P, N_PASSES * P], U8, name="rw_scale%d" % i, align_bytes=MX_ALIGN)
            sources = quarters(rw_sorted[i][:].bitcast(F32))
            turn_over(("rewritten", i), sources, rw_codes[i][:], rw_scale[i][:], E5M2X4)

        def spread_prior(part):
            bank = new_bank()
            words = prior_rows[:].bitcast(F32)
            for c in range(4):
                column = words[:, 4 * part + c : 4 * part + c + 1]
                nc.tensor.transpose(bank[:, c * P : (c + 1) * P], column.to_broadcast([P, P]), ident[:])
            nc.scalar.copy(
                out=prior_all[:].bitcast(F32).rearrange("m (p c) -> m p c", c=8)[:, :, 4 * part : 4 * part + 4],
                in_=bank[:].rearrange("m (c p) -> m p c", c=4),
            )

        def delta_pass(bank, i, half, g):
            for first in range(g + 1):
                quantise_up_to(("context", i, first))
            nc.tensor.matmul_mx(
                out=bank[:],
                lhsT=ctx_codes[i, g].bitcast(E4M3X4),
                lhsT_scale=ctx_scale[i, g],
                rhs=w_codes[g][:, 2 * BANK * half : 2 * BANK * (half + 1)].bitcast(E2M1X4),
                rhs_scale=w_scale[:, g * N + BANK * half : g * N + BANK * (half + 1)],
                start=(g == 0),
                stop=(g == K_PASSES - 1),
            )

        def delta_half(i, half):
            bank = new_bank()
            for g in range(K_PASSES):
                delta_pass(bank, i, half, g)
            return bank

        def rewrite(bank, i, half):
            if half == 0:
                rw_sorted[i] = work.tile([P, N], BF16, name="rw_sorted", tag="rw_sorted", bufs=REWRITTEN_BUFS)
            cols = slice(half * BANK, (half + 1) * BANK)
            for u in range(2):
                nc.vector.scalar_tensor_tensor(
                    out=rw_sorted[i][:, cols].rearrange("p (u b x) -> p u b x", u=2, x=16)[:, u],
                    in0=bank[:].rearrange("p (b u x) -> p u b x", u=2, x=16)[:, u],
                    scalar=gate_cols[:, i : i + 1],
                    in1=turn_raw[i][:, cols].rearrange("p (b u x) -> p u b x", u=2, x=16)[:, u],
                    op0=MULT,
                    op1=ADD,
                )

        scored = []

        def score(patches):
            for i, j in patches:
                scored.append((i, j))
                quantise_up_to(("rewritten", i))
                quantise_up_to(("docs", j))
                bank = new_bank()
                for g in range(N_PASSES):
                    nc.tensor.matmul_mx(
                        out=bank[:],
                        lhsT=rw_codes[i][:, g * P : (g + 1) * P].bitcast(E5M2X4),
                        lhsT_scale=rw_scale[i][:, g * P : (g + 1) * P],
                        rhs=doc_codes[j, g][:].bitcast(E4M3X4),
                        rhs_scale=doc_scale[j, g][:],
                        start=(g == 0),
                        stop=(g == N_PASSES - 1),
                    )
                parts = LAST_STORES if len(scored) == M_TILES * D_CHUNKS else 1
                width = BANK // parts
                for part in range(parts):
                    cols = slice(j * BANK + part * width, j * BANK + (part + 1) * width)
                    scores = work.tile([P, width], F32, name="scores", tag="scores", bufs=SCORE_BUFS)
                    nc.vector.tensor_tensor(
                        out=scores[:], in0=bank[:, part * width : (part + 1) * width], in1=prior_all[:, cols], op=ADD
                    )
                    nc.sync.dma_start(out=out_rows[i][:, cols], in_=scores[:])
                quantise_pending(1)

        def open_patches(tiles, last_doc_step):
            chunks = min(last_doc_step - FIRST_DOC_STEP + 1, D_CHUNKS)
            return [(i, j) for i in range(tiles) for j in range(chunks) if (i, j) not in scored]

        def pieces_on_scalar(s):
            return DOC_PIECES_ON_SCALAR if s > FIRST_DOC_STEP else 0

        turn_context(0, (0,))
        spread_prior(0)
        sort_context(0, nc.vector.tensor_copy, PASS_PAIRS[1:])
        quantise_pending(1)
        turn_context(0, (1,))
        turn_context(0, (2, 3))
        banks = [new_bank(), new_bank()]
        for g in PASS_PAIRS[0]:
            for half in range(2):
                delta_pass(banks[half], 0, half, g)
        quantise_pending(1)
        for passes in PASS_PAIRS:
            turn_context(1, passes)
        for g in PASS_PAIRS[1]:
            for half in range(2):
                delta_pass(banks[half], 0, half, g)
        sort_context(2, nc.scalar.copy)
        quantise_pending(2)
        for half in range(2):
            rewrite(banks[half], 0, half)

        for s in range(1, M_TILES):
            last = s + 1 == M_TILES
            sort_docs(doc_pieces(s)[pieces_on_scalar(s) :], nc.vector.tensor_copy)
            bank = delta_half(s, 0)
            quantise_pending(N_PASSES)
            rewrite(bank, s, 0)
            patches = open_patches(s - 1, s - 2)
            score(patches[: (len(patches) + 1) // 2])

            if not last:
                for passes in PASS_PAIRS:
                    turn_context(s + 1, passes)
            turn_rewritten(s - 1)
            if s == 1:
                spread_prior(1)
            if doc_pieces(s):
                for g in range(N_PASSES):
                    turn_docs(s - FIRST_DOC_STEP, g)
            if LAST_CONTEXT_ON_VECTOR < s + 2 < M_TILES:
                sort_context(s + 2, nc.scalar.copy)

            bank = delta_half(s, 1)
            quantise_pending(len(PASS_PAIRS))
            if s + 2 <= LAST_CONTEXT_ON_VECTOR:
                sort_context(s + 2, nc.vector.tensor_copy)
            quantise_pending(1)
            rewrite(bank, s, 1)
            if last:
                score(open_patches(s, s)[:-HELD_BACK])
            else:
                score(open_patches(s - 1, s - 1))
            sort_docs(doc_pieces(s + 1)[: pieces_on_scalar(s + 1)], nc.scalar.copy)

        turn_rewritten(M_TILES - 1)
        score(open_patches(M_TILES, M_TILES))
